import numpy as np
import ml_dtypes


def mxq(x, axis, fmt="e4m3"):
    dtype, down = {"e4m3": (ml_dtypes.float8_e4m3fn, 7), "e5m2": (ml_dtypes.float8_e5m2, 14)}[fmt]
    v = np.moveaxis(np.asarray(x, np.float32).astype(ml_dtypes.bfloat16).astype(np.float64), axis, -1)
    blocks = v.reshape(v.shape[:-1] + (-1, 32))
    amax = np.abs(blocks).max(-1, keepdims=True)
    byte = np.maximum(np.where(amax > 0, np.frexp(amax)[1] - 1 + 127, 0) - down, 1)
    scale = np.exp2(byte - 127.0)
    codes = (blocks / scale).astype(np.float32).astype(dtype).astype(np.float64)
    return np.moveaxis((codes * scale).reshape(v.shape), -1, axis)


WIDE = False


def mx_kscale(k):
    if not WIDE:
        return np.ones(k)
    levels = np.array([10, -10, 5, -5, 0])
    if k % 512:
        return np.exp2(np.random.permutation(np.resize(levels, k // 32))).repeat(32)
    a = np.empty((k // 512, 16))
    for p in range(k // 512):
        a[p, :8] = np.random.permutation(np.resize(levels, 8))
        for g in range(8):
            far = levels[np.abs(levels - a[p, g]) >= 10]
            a[p, g + 8] = far[np.random.randint(len(far))]
    return np.exp2(a.ravel()).repeat(32)


def f64(x):
    return np.asarray(x).astype(np.float64)


def striped(idx):
    return np.tile(idx.reshape(-1, 16).T, (8, 1)).astype(np.uint16)


def unstriped(offs):
    return offs[:16].T.reshape(-1).astype(np.int64)


def pack_weight(w):
    k, n = w.shape
    w = f64(np.asarray(w, np.float32).astype(ml_dtypes.bfloat16)).reshape(k // 32, 32, n)
    amax = np.abs(w).max(1)
    byte = np.clip(np.where(amax > 0, np.frexp(amax)[1] - 1 + 127 - 7, 1), 1, 254)
    scaled = (w * np.exp2(127.0 - byte)[:, None, :]).reshape(k, n).astype(np.float32)
    words = np.ascontiguousarray(scaled.reshape(k // 512, 128, 4, n).transpose(0, 1, 3, 2)).astype(ml_dtypes.float8_e4m3fn).view(np.uint8)
    return words, np.ascontiguousarray(byte.astype(np.uint8).reshape(k // 512, 16, n))


def unpack_weight(words, scales):
    g, p, n, _ = words.shape
    vals = np.ascontiguousarray(words).view(ml_dtypes.float8_e4m3fn).astype(np.float64) * np.repeat(np.exp2(scales.astype(np.float64) - 127.0), 8, axis=1)[..., None]
    return vals.transpose(0, 1, 3, 2).reshape(g * 512, n)


def relu(v):
    return np.maximum(v, 0.0)


K, T, S, V = 512, 2048, 512, 512


def setup_inputs():
    n = np.random.standard_normal
    s = mx_kscale(K)[:, None]
    packed_xT = pack_weight(n((K, T)) * s)
    return {
        "x_words": packed_xT[0],
        "x_scales": packed_xT[1],
        "hT": (n((K, V)) / np.sqrt(K) / s).astype(np.float32),
        "offs": striped(np.random.permutation(T)[:S]),
    }


def reference(x_words, x_scales, hT, offs):
    hTq = mxq(f64(hT), 0, "e4m3")
    xq = unpack_weight(x_words, x_scales)[:, unstriped(offs)]
    y = hTq.T @ xq
    ex = np.exp(y - y.max(axis=1, keepdims=True))
    p = ex / ex.sum(axis=1, keepdims=True)
    top = p.max(axis=1, keepdims=True)
    rr = relu(p - (0.02 * top))
    total = rr.sum(axis=1, keepdims=True)
    return rr / total

@@ -1,0 +1,123 @@
+from contextlib import ExitStack
+
+import concourse.mybir as mybir
+
+K, T, S, V = 512, 2048, 512, 512
+FLOPS = 2 * K * S * V
+F32 = mybir.dt.float32
+BF16 = mybir.dt.bfloat16
+I32 = mybir.dt.int32
+U32 = mybir.dt.uint32
+U16 = mybir.dt.uint16
+U8 = mybir.dt.uint8
+FP8X4 = mybir.dt.float8_e4m3fn_x4
+ALU = mybir.AluOpType
+ACT = mybir.ActivationFunctionType
+AX = mybir.AxisListType
+P = 128
+C = 0.02
+
+
+def tile_picked_yminp_minp_p_kernel(tc, x_words, x_scales, hT, offs, out):
+    nc = tc.nc
+    with ExitStack() as ctx:
+        keep = ctx.enter_context(tc.tile_pool(name="keep", bufs=1))
+        psum = ctx.enter_context(tc.psum_pool(name="psum", bufs=1))
+
+        offsets = keep.tile([P, S // 16], U16, name="offsets")
+        words = keep.tile([P, T], U32, name="words", align_bytes=64)
+        scal = keep.tile([P, T], U8, name="scal", align_bytes=64)
+        xw = keep.tile([P, S], U32, name="xw", align_bytes=64)
+        xs = keep.tile([P, S], U8, name="xs", align_bytes=64)
+        raw = [keep.tile([P, 4, 256], F32, name="raw%d" % h, align_bytes=64) for h in range(2)]
+        grp = [keep.tile([P, 128, 4], BF16, name="grp%d" % i, align_bytes=64) for i in range(4)]
+        hw = [keep.tile([P, 128], U32, name="hw%d" % i, align_bytes=64) for i in range(4)]
+        hs = [keep.tile([P, 128], U8, name="hs%d" % i, align_bytes=64) for i in range(4)]
+        y = [psum.tile([P, S], F32, name="y%d" % i) for i in range(4)]
+        nmax = [keep.tile([P, 1], F32, name="nmax%d" % i) for i in range(4)]
+        tot = [keep.tile([P, 1], F32, name="tot%d" % i) for i in range(4)]
+        rec = [keep.tile([P, 1], F32, name="rec%d" % i) for i in range(4)]
+        e = [keep.tile([P, S], F32, name="e%d" % i, align_bytes=64) for i in range(4)]
+        r = [keep.tile([P, S], F32, name="r%d" % i, align_bytes=64) for i in range(4)]
+        o = [keep.tile([P, S], F32, name="o%d" % i, align_bytes=64) for i in range(4)]
+        warm = keep.tile([P, 1], F32, name="warm")
+        warm2 = keep.tile([P, 1], F32, name="warm2")
+
+        hv = hT.rearrange("(p j) t -> p j t", j=4)
+        nc.vector.memset(scal[:].bitcast(I32), 0)
+        nc.gpsimd.memset(warm[:], 0.0)
+        nc.sync.dma_start(offsets[:], offs)
+        for q in range(4):
+            nc.scalar.dma_start(out=scal[32 * q : 32 * q + 4, :].bitcast(I32), in_=x_scales[0, 4 * q : 4 * q + 4, :].bitcast(I32))
+        nc.scalar.activation(out=warm2[:], in_=warm[:], func=ACT.Exp)
+        nc.sync.dma_start(out=raw[0][:], in_=hv[:, :, 0:256])
+        nc.sync.dma_start(out=words[:].bitcast(I32), in_=x_words[0].rearrange("p n t -> p (n t)").bitcast(I32))
+        nc.sync.dma_start(out=raw[1][:], in_=hv[:, :, 256:512])
+
+        def cast(i, on_vector):
+            src = raw[i // 2][:, :, 128 * (i % 2) : 128 * (i % 2) + 128].rearrange("p j (c i) -> p c j i", i=4)
+            dst = grp[i][:].rearrange("p (c i) j -> p c j i", i=4)
+            if on_vector:
+                nc.vector.tensor_copy(out=dst, in_=src)
+            else:
+                nc.scalar.copy(out=dst, in_=src)
+
+        def quant(i):
+            nc.vector.quantize_mx(out=hw[i][:].bitcast(FP8X4), scales=hs[i][:], in_=grp[i][:].rearrange("p c j -> p (c j)"))
+
+        def mm(i):
+            nc.tensor.matmul_mx(out=y[i][:], lhsT=hw[i][:].bitcast(FP8X4), lhsT_scale=hs[i][:], rhs=xw[:].bitcast(FP8X4), rhs_scale=xs[:], start=True, stop=True)
+
+        def rowmax(i):
+            nc.vector.tensor_reduce(out=nmax[i][:], in_=y[i][:], axis=AX.X, op=ALU.max, negate=True)
+
+        def expo(i):
+            nc.scalar.activation(out=e[i][:], in_=y[i][:], func=ACT.Exp, bias=nmax[i][:], scale=1.0)
+
+        def keep_s(i):
+            nc.scalar.activation(out=r[i][:], in_=e[i][:], func=ACT.Relu, bias=-C, scale=1.0, accum_out=tot[i][:])
+
+        def keep_v(i):
+            nc.vector.tensor_scalar(out=r[i][:], in0=e[i][:], scalar1=C, scalar2=-C * S, op0=ALU.max, op1=ALU.add, accum_out=tot[i][:])
+
+        def recip(i):
+            nc.vector.reciprocal(out=rec[i][:], in_=tot[i][:])
+
+        def norm(i, shifted):
+            nc.vector.tensor_scalar(out=o[i][:], in0=r[i][:], scalar1=(-C if shifted else 0.0), scalar2=rec[i][:], op0=ALU.add, op1=ALU.mult)
+            nc.sync.dma_start(out=out[128 * i : 128 * i + 128, :], in_=o[i][:])
+
+        nc.vector.tensor_copy(out=xs[:], in_=scal[:].indirect(offsets[:]))
+        cast(0, False)
+        cast(1, False)
+        quant(0)
+        quant(1)
+        nc.vector.tensor_copy(out=xw[:], in_=words[:].indirect(offsets[:]))
+        mm(0)
+        mm(1)
+        cast(2, True)
+        cast(3, False)
+        rowmax(0)
+        expo(0)
+        quant(2)
+        quant(3)
+        mm(2)
+        mm(3)
+        rowmax(1)
+        keep_s(0)
+        expo(1)
+        rowmax(2)
+        recip(0)
+        keep_s(1)
+        expo(2)
+        norm(0, False)
+        rowmax(3)
+        recip(1)
+        keep_s(2)
+        expo(3)
+        norm(1, False)
+        recip(2)
+        keep_v(3)
+        norm(2, False)
+        recip(3)
+        norm(3, True)

@@ -4,6 +4,8 @@ import concourse.mybir as mybir
 
 K, T, S, V = 512, 2048, 512, 512
 FLOPS = 2 * K * S * V
+MIN_P = 0.02
+
 F32 = mybir.dt.float32
 BF16 = mybir.dt.bfloat16
 I32 = mybir.dt.int32
@@ -13,9 +15,16 @@ U8 = mybir.dt.uint8
 FP8X4 = mybir.dt.float8_e4m3fn_x4
 ALU = mybir.AluOpType
 ACT = mybir.ActivationFunctionType
-AX = mybir.AxisListType
+AXIS = mybir.AxisListType
+
 P = 128
-C = 0.02
+PACK = 4
+TILES = V // P
+QUADRANT = 32
+
+WORDS_AHEAD = 640
+H_LOADS = ((0,), (1, 2), (3,))
+VECTOR_TILE = 1
 
 
 def tile_picked_yminp_minp_p_kernel(tc, x_words, x_scales, hT, offs, out):
@@ -24,100 +33,124 @@ def tile_picked_yminp_minp_p_kernel(tc, x_words, x_scales, hT, offs, out):
         keep = ctx.enter_context(tc.tile_pool(name="keep", bufs=1))
         psum = ctx.enter_context(tc.psum_pool(name="psum", bufs=1))
 
+        def per_tile(name, shape, dtype):
+            return [keep.tile(shape, dtype, name="%s%d" % (name, i), align_bytes=64) for i in range(TILES)]
+
         offsets = keep.tile([P, S // 16], U16, name="offsets")
-        words = keep.tile([P, T], U32, name="words", align_bytes=64)
-        scal = keep.tile([P, T], U8, name="scal", align_bytes=64)
-        xw = keep.tile([P, S], U32, name="xw", align_bytes=64)
-        xs = keep.tile([P, S], U8, name="xs", align_bytes=64)
-        raw = [keep.tile([P, 4, 256], F32, name="raw%d" % h, align_bytes=64) for h in range(2)]
-        grp = [keep.tile([P, 128, 4], BF16, name="grp%d" % i, align_bytes=64) for i in range(4)]
-        hw = [keep.tile([P, 128], U32, name="hw%d" % i, align_bytes=64) for i in range(4)]
-        hs = [keep.tile([P, 128], U8, name="hs%d" % i, align_bytes=64) for i in range(4)]
-        y = [psum.tile([P, S], F32, name="y%d" % i) for i in range(4)]
-        nmax = [keep.tile([P, 1], F32, name="nmax%d" % i) for i in range(4)]
-        tot = [keep.tile([P, 1], F32, name="tot%d" % i) for i in range(4)]
-        rec = [keep.tile([P, 1], F32, name="rec%d" % i) for i in range(4)]
-        e = [keep.tile([P, S], F32, name="e%d" % i, align_bytes=64) for i in range(4)]
-        r = [keep.tile([P, S], F32, name="r%d" % i, align_bytes=64) for i in range(4)]
-        o = [keep.tile([P, S], F32, name="o%d" % i, align_bytes=64) for i in range(4)]
-        warm = keep.tile([P, 1], F32, name="warm")
-        warm2 = keep.tile([P, 1], F32, name="warm2")
+        table_words = keep.tile([P, T], U32, name="table_words", align_bytes=64)
+        table_scales = keep.tile([P, T], U8, name="table_scales", align_bytes=64)
+        picked_words = keep.tile([P, S], U32, name="picked_words", align_bytes=64)
+        picked_scales = keep.tile([P, S], U8, name="picked_scales", align_bytes=64)
+        h_loaded = [
+            keep.tile([P, PACK, P * len(tiles)], F32, name="h_loaded%d" % n, align_bytes=64)
+            for n, tiles in enumerate(H_LOADS)
+        ]
+        h_raw = [h_loaded[n][:, :, P * m : P * (m + 1)] for n, tiles in enumerate(H_LOADS) for m in range(len(tiles))]
+        h_bf16 = per_tile("h_bf16", [P, P, PACK], BF16)
+        h_words = per_tile("h_words", [P, P], U32)
+        h_scales = per_tile("h_scales", [P, P], U8)
+        scores = [psum.tile([P, S], F32, name="scores%d" % i) for i in range(TILES)]
+        exps = per_tile("exps", [P, S], F32)
+        kept = per_tile("kept", [P, S], F32)
+        result = per_tile("result", [P, S], F32)
+        total = per_tile("total", [P, 1], F32)
+        inverse = per_tile("inverse", [P, 1], F32)
+        neg_max = [h_bf16[VECTOR_TILE][:, 0, 0:2].bitcast(F32)] + [
+            keep.tile([P, 1], F32, name="neg_max%d" % i)[:] for i in range(1, TILES)
+        ]
+        zero = keep.tile([P, 1], F32, name="zero")
+        top = keep.tile([P, 1], F32, name="top")
+        floor = keep.tile([P, 1], F32, name="floor")
+        neg_floor = keep.tile([P, 1], F32, name="neg_floor")
+        neg_floors = keep.tile([P, 1], F32, name="neg_floors")
 
-        hv = hT.rearrange("(p j) t -> p j t", j=4)
-        nc.vector.memset(scal[:].bitcast(I32), 0)
-        nc.gpsimd.memset(warm[:], 0.0)
+        nc.vector.memset(table_scales[:].bitcast(I32), 0)
+        nc.gpsimd.memset(zero[:], 0.0)
+
+        words_hbm = x_words[0].rearrange("p c j -> p (c j)").bitcast(I32)
+        nc.sync.dma_start(out=table_words[:, :WORDS_AHEAD].bitcast(I32), in_=words_hbm[:, :WORDS_AHEAD])
         nc.sync.dma_start(offsets[:], offs)
-        for q in range(4):
-            nc.scalar.dma_start(out=scal[32 * q : 32 * q + 4, :].bitcast(I32), in_=x_scales[0, 4 * q : 4 * q + 4, :].bitcast(I32))
-        nc.scalar.activation(out=warm2[:], in_=warm[:], func=ACT.Exp)
-        nc.sync.dma_start(out=raw[0][:], in_=hv[:, :, 0:256])
-        nc.sync.dma_start(out=words[:].bitcast(I32), in_=x_words[0].rearrange("p n t -> p (n t)").bitcast(I32))
-        nc.sync.dma_start(out=raw[1][:], in_=hv[:, :, 256:512])
+        for r in range(PACK):
+            nc.sync.dma_start(out=table_scales[r:P:QUADRANT, :].bitcast(I32), in_=x_scales[0, r : K // 32 : 4, :].bitcast(I32))
+        nc.sync.dma_start(out=table_words[:, WORDS_AHEAD:].bitcast(I32), in_=words_hbm[:, WORDS_AHEAD:])
+        h_hbm = hT.rearrange("(p j) t -> p j t", j=PACK)
+        for n, tiles in enumerate(H_LOADS):
+            nc.sync.dma_start(out=h_loaded[n][:], in_=h_hbm[:, :, P * tiles[0] : P * (tiles[-1] + 1)])
 
-        def cast(i, on_vector):
-            src = raw[i // 2][:, :, 128 * (i % 2) : 128 * (i % 2) + 128].rearrange("p j (c i) -> p c j i", i=4)
-            dst = grp[i][:].rearrange("p (c i) j -> p c j i", i=4)
-            if on_vector:
+        nc.scalar.activation(out=top[:], in_=zero[:], func=ACT.Exp)
+        nc.scalar.activation(out=floor[:], in_=top[:], func=ACT.Copy, scale=MIN_P)
+        nc.scalar.activation(out=neg_floor[:], in_=top[:], func=ACT.Copy, scale=-MIN_P)
+        nc.scalar.activation(out=neg_floors[:], in_=top[:], func=ACT.Copy, scale=-MIN_P * S)
+
+        def round_to_bf16(i):
+            src = h_raw[i].rearrange("p j (c n) -> p c j n", n=4)
+            dst = h_bf16[i][:].rearrange("p (c n) j -> p c j n", n=4)
+            if i == VECTOR_TILE:
                 nc.vector.tensor_copy(out=dst, in_=src)
             else:
                 nc.scalar.copy(out=dst, in_=src)
 
-        def quant(i):
-            nc.vector.quantize_mx(out=hw[i][:].bitcast(FP8X4), scales=hs[i][:], in_=grp[i][:].rearrange("p c j -> p (c j)"))
+        def quantise_and_multiply(i):
+            nc.vector.quantize_mx(
+                out=h_words[i][:].bitcast(FP8X4), scales=h_scales[i][:], in_=h_bf16[i][:].rearrange("p t j -> p (t j)")
+            )
+            nc.tensor.matmul_mx(
+                out=scores[i][:],
+                lhsT=h_words[i][:].bitcast(FP8X4),
+                lhsT_scale=h_scales[i][:],
+                rhs=picked_words[:].bitcast(FP8X4),
+                rhs_scale=picked_scales[:],
+                start=True,
+                stop=True,
+            )
 
-        def mm(i):
-            nc.tensor.matmul_mx(out=y[i][:], lhsT=hw[i][:].bitcast(FP8X4), lhsT_scale=hs[i][:], rhs=xw[:].bitcast(FP8X4), rhs_scale=xs[:], start=True, stop=True)
+        def exponentiate(i):
+            nc.vector.tensor_reduce(out=neg_max[i], in_=scores[i][:], axis=AXIS.X, op=ALU.max, negate=True)
+            nc.scalar.activation(out=exps[i][:], in_=scores[i][:], func=ACT.Exp, bias=neg_max[i], scale=1.0)
 
-        def rowmax(i):
-            nc.vector.tensor_reduce(out=nmax[i][:], in_=y[i][:], axis=AX.X, op=ALU.max, negate=True)
+        def threshold(i):
+            if i == VECTOR_TILE:
+                nc.vector.tensor_scalar(
+                    out=kept[i][:], in0=exps[i][:], scalar1=floor[:], scalar2=neg_floors[:],
+                    op0=ALU.max, op1=ALU.add, accum_out=total[i][:],
+                )
+            else:
+                nc.scalar.activation(
+                    out=kept[i][:], in_=exps[i][:], func=ACT.Relu, bias=neg_floor[:], scale=1.0, accum_out=total[i][:]
+                )
 
-        def expo(i):
-            nc.scalar.activation(out=e[i][:], in_=y[i][:], func=ACT.Exp, bias=nmax[i][:], scale=1.0)
+        def invert(i):
+            nc.vector.reciprocal(out=inverse[i][:], in_=total[i][:])
 
-        def keep_s(i):
-            nc.scalar.activation(out=r[i][:], in_=e[i][:], func=ACT.Relu, bias=-C, scale=1.0, accum_out=tot[i][:])
+        def normalise_and_store(i):
+            if i == VECTOR_TILE:
+                nc.vector.tensor_scalar(
+                    out=result[i][:], in0=kept[i][:], scalar1=neg_floor[:], scalar2=inverse[i][:], op0=ALU.add, op1=ALU.mult
+                )
+            else:
+                nc.vector.tensor_scalar(
+                    out=result[i][:], in0=kept[i][:], scalar1=inverse[i][:], scalar2=None, op0=ALU.mult
+                )
+            nc.sync.dma_start(out=out[P * i : P * (i + 1), :], in_=result[i][:])
 
-        def keep_v(i):
-            nc.vector.tensor_scalar(out=r[i][:], in0=e[i][:], scalar1=C, scalar2=-C * S, op0=ALU.max, op1=ALU.add, accum_out=tot[i][:])
+        nc.vector.tensor_copy(out=picked_scales[:], in_=table_scales[:].indirect(offsets[:]))
+        nc.vector.tensor_copy(out=picked_words[:], in_=table_words[:].indirect(offsets[:]))
 
-        def recip(i):
-            nc.vector.reciprocal(out=rec[i][:], in_=tot[i][:])
-
-        def norm(i, shifted):
-            nc.vector.tensor_scalar(out=o[i][:], in0=r[i][:], scalar1=(-C if shifted else 0.0), scalar2=rec[i][:], op0=ALU.add, op1=ALU.mult)
-            nc.sync.dma_start(out=out[128 * i : 128 * i + 128, :], in_=o[i][:])
-
-        nc.vector.tensor_copy(out=xs[:], in_=scal[:].indirect(offsets[:]))
-        cast(0, False)
-        cast(1, False)
-        quant(0)
-        quant(1)
-        nc.vector.tensor_copy(out=xw[:], in_=words[:].indirect(offsets[:]))
-        mm(0)
-        mm(1)
-        cast(2, True)
-        cast(3, False)
-        rowmax(0)
-        expo(0)
-        quant(2)
-        quant(3)
-        mm(2)
-        mm(3)
-        rowmax(1)
-        keep_s(0)
-        expo(1)
-        rowmax(2)
-        recip(0)
-        keep_s(1)
-        expo(2)
-        norm(0, False)
-        rowmax(3)
-        recip(1)
-        keep_s(2)
-        expo(3)
-        norm(1, False)
-        recip(2)
-        keep_v(3)
-        norm(2, False)
-        recip(3)
-        norm(3, True)
+        for i in (0, 1):
+            round_to_bf16(i)
+            quantise_and_multiply(i)
+        for i in (2, 3):
+            round_to_bf16(i)
+        exponentiate(0)
+        for i in (2, 3):
+            quantise_and_multiply(i)
+        threshold(0)
+        invert(0)
+        for i in range(1, TILES):
+            exponentiate(i)
+        for i in range(1, TILES):
+            threshold(i)
+        normalise_and_store(0)
+        for i in range(1, TILES):
+            invert(i)
+            normalise_and_store(i)

from contextlib import ExitStack

import concourse.mybir as mybir

K, T, S, V = 512, 2048, 512, 512
FLOPS = 2 * K * S * V
MIN_P = 0.02

F32 = mybir.dt.float32
BF16 = mybir.dt.bfloat16
I32 = mybir.dt.int32
U32 = mybir.dt.uint32
U16 = mybir.dt.uint16
U8 = mybir.dt.uint8
FP8X4 = mybir.dt.float8_e4m3fn_x4
ALU = mybir.AluOpType
ACT = mybir.ActivationFunctionType
AXIS = mybir.AxisListType

P = 128
PACK = 4
TILES = V // P
QUADRANT = 32

WORDS_AHEAD = 640
H_LOADS = ((0,), (1, 2), (3,))
VECTOR_TILE = 1


def tile_picked_yminp_minp_p_kernel(tc, x_words, x_scales, hT, offs, out):
    nc = tc.nc
    with ExitStack() as ctx:
        keep = ctx.enter_context(tc.tile_pool(name="keep", bufs=1))
        psum = ctx.enter_context(tc.psum_pool(name="psum", bufs=1))

        def per_tile(name, shape, dtype):
            return [keep.tile(shape, dtype, name="%s%d" % (name, i), align_bytes=64) for i in range(TILES)]

        offsets = keep.tile([P, S // 16], U16, name="offsets")
        table_words = keep.tile([P, T], U32, name="table_words", align_bytes=64)
        table_scales = keep.tile([P, T], U8, name="table_scales", align_bytes=64)
        picked_words = keep.tile([P, S], U32, name="picked_words", align_bytes=64)
        picked_scales = keep.tile([P, S], U8, name="picked_scales", align_bytes=64)
        h_loaded = [
            keep.tile([P, PACK, P * len(tiles)], F32, name="h_loaded%d" % n, align_bytes=64)
            for n, tiles in enumerate(H_LOADS)
        ]
        h_raw = [h_loaded[n][:, :, P * m : P * (m + 1)] for n, tiles in enumerate(H_LOADS) for m in range(len(tiles))]
        h_bf16 = per_tile("h_bf16", [P, P, PACK], BF16)
        h_words = per_tile("h_words", [P, P], U32)
        h_scales = per_tile("h_scales", [P, P], U8)
        scores = [psum.tile([P, S], F32, name="scores%d" % i) for i in range(TILES)]
        exps = per_tile("exps", [P, S], F32)
        kept = per_tile("kept", [P, S], F32)
        result = per_tile("result", [P, S], F32)
        total = per_tile("total", [P, 1], F32)
        inverse = per_tile("inverse", [P, 1], F32)
        neg_max = [h_bf16[VECTOR_TILE][:, 0, 0:2].bitcast(F32)] + [
            keep.tile([P, 1], F32, name="neg_max%d" % i)[:] for i in range(1, TILES)
        ]
        zero = keep.tile([P, 1], F32, name="zero")
        top = keep.tile([P, 1], F32, name="top")
        floor = keep.tile([P, 1], F32, name="floor")
        neg_floor = keep.tile([P, 1], F32, name="neg_floor")
        neg_floors = keep.tile([P, 1], F32, name="neg_floors")

        nc.vector.memset(table_scales[:].bitcast(I32), 0)
        nc.gpsimd.memset(zero[:], 0.0)

        words_hbm = x_words[0].rearrange("p c j -> p (c j)").bitcast(I32)
        nc.sync.dma_start(out=table_words[:, :WORDS_AHEAD].bitcast(I32), in_=words_hbm[:, :WORDS_AHEAD])
        nc.sync.dma_start(offsets[:], offs)
        for r in range(PACK):
            nc.sync.dma_start(out=table_scales[r:P:QUADRANT, :].bitcast(I32), in_=x_scales[0, r : K // 32 : 4, :].bitcast(I32))
        nc.sync.dma_start(out=table_words[:, WORDS_AHEAD:].bitcast(I32), in_=words_hbm[:, WORDS_AHEAD:])
        h_hbm = hT.rearrange("(p j) t -> p j t", j=PACK)
        for n, tiles in enumerate(H_LOADS):
            nc.sync.dma_start(out=h_loaded[n][:], in_=h_hbm[:, :, P * tiles[0] : P * (tiles[-1] + 1)])

        nc.scalar.activation(out=top[:], in_=zero[:], func=ACT.Exp)
        nc.scalar.activation(out=floor[:], in_=top[:], func=ACT.Copy, scale=MIN_P)
        nc.scalar.activation(out=neg_floor[:], in_=top[:], func=ACT.Copy, scale=-MIN_P)
        nc.scalar.activation(out=neg_floors[:], in_=top[:], func=ACT.Copy, scale=-MIN_P * S)

        def round_to_bf16(i):
            src = h_raw[i].rearrange("p j (c n) -> p c j n", n=4)
            dst = h_bf16[i][:].rearrange("p (c n) j -> p c j n", n=4)
            if i == VECTOR_TILE:
                nc.vector.tensor_copy(out=dst, in_=src)
            else:
                nc.scalar.copy(out=dst, in_=src)

        def quantise_and_multiply(i):
            nc.vector.quantize_mx(
                out=h_words[i][:].bitcast(FP8X4), scales=h_scales[i][:], in_=h_bf16[i][:].rearrange("p t j -> p (t j)")
            )
            nc.tensor.matmul_mx(
                out=scores[i][:],
                lhsT=h_words[i][:].bitcast(FP8X4),
                lhsT_scale=h_scales[i][:],
                rhs=picked_words[:].bitcast(FP8X4),
                rhs_scale=picked_scales[:],
                start=True,
                stop=True,
            )

        def exponentiate(i):
            nc.vector.tensor_reduce(out=neg_max[i], in_=scores[i][:], axis=AXIS.X, op=ALU.max, negate=True)
            nc.scalar.activation(out=exps[i][:], in_=scores[i][:], func=ACT.Exp, bias=neg_max[i], scale=1.0)

        def threshold(i):
            if i == VECTOR_TILE:
                nc.vector.tensor_scalar(
                    out=kept[i][:], in0=exps[i][:], scalar1=floor[:], scalar2=neg_floors[:],
                    op0=ALU.max, op1=ALU.add, accum_out=total[i][:],
                )
            else:
                nc.scalar.activation(
                    out=kept[i][:], in_=exps[i][:], func=ACT.Relu, bias=neg_floor[:], scale=1.0, accum_out=total[i][:]
                )

        def invert(i):
            nc.vector.reciprocal(out=inverse[i][:], in_=total[i][:])

        def normalise_and_store(i):
            if i == VECTOR_TILE:
                nc.vector.tensor_scalar(
                    out=result[i][:], in0=kept[i][:], scalar1=neg_floor[:], scalar2=inverse[i][:], op0=ALU.add, op1=ALU.mult
                )
            else:
                nc.vector.tensor_scalar(
                    out=result[i][:], in0=kept[i][:], scalar1=inverse[i][:], scalar2=None, op0=ALU.mult
                )
            nc.sync.dma_start(out=out[P * i : P * (i + 1), :], in_=result[i][:])

        nc.vector.tensor_copy(out=picked_scales[:], in_=table_scales[:].indirect(offsets[:]))
        nc.vector.tensor_copy(out=picked_words[:], in_=table_words[:].indirect(offsets[:]))

        for i in (0, 1):
            round_to_bf16(i)
            quantise_and_multiply(i)
        for i in (2, 3):
            round_to_bf16(i)
        exponentiate(0)
        for i in (2, 3):
            quantise_and_multiply(i)
        threshold(0)
        invert(0)
        for i in range(1, TILES):
            exponentiate(i)
        for i in range(1, TILES):
            threshold(i)
        normalise_and_store(0)
        for i in range(1, TILES):
            invert(i)
            normalise_and_store(i)
